import numpy as np, ml_dtypes
CORES = [2,10,34,50,74,82,98,114,130,138,162,178,202,210,226,242]
N = 16
DEG, TK, TIMES = 16, 128, 2
MASK = [[0,1,2,3,4,5,6,7,8,9,10,11,12,13,14,15],[0,1,2,3,4,5,6,7,8,9,10,11,12,13,14,15],[0,1,2,3,4,5,6,7,8,9,10,11,12,13,14,15],[0,1,2,3,4,5,6,7,8,9,10,11,12,13,14,15],[0,1,2,3,4,5,6,7,8,9,10,11,12,13,14,15],[0,1,2,3,4,5,6,7,8,9,10,11,12,13,14,15],[0,1,2,3,4,5,6,7,8,9,10,11,12,13,14,15],[0,1,2,3,4,5,6,7,8,9,10,11,12,13,14,15],[0,1,2,3,4,5,6,7,8,9,10,11,12,13,14,15],[0,1,2,3,4,5,6,7,8,9,10,11,12,13,14,15],[0,1,2,3,4,5,6,7,8,9,10,11,12,13,14,15],[0,1,2,3,4,5,6,7,8,9,10,11,12,13,14,15],[0,1,2,3,4,5,6,7,8,9,10,11,12,13,14,15],[0,1,2,3,4,5,6,7,8,9,10,11,12,13,14,15],[0,1,2,3,4,5,6,7,8,9,10,11,12,13,14,15],[0,1,2,3,4,5,6,7,8,9,10,11,12,13,14,15]]
def setup_inputs(rng):
    return {"x": rng.standard_normal((N, 128, TK), dtype=np.float32).astype(ml_dtypes.bfloat16), "w": (rng.standard_normal((N, 128, DEG * 128), dtype=np.float32) / np.float32(np.sqrt(128 * DEG / 2))).astype(ml_dtypes.bfloat16)}
def setup_inputs_big(rng):
    d = setup_inputs(rng)
    for k in ("x",): d[k] = (d[k].astype(np.float32) * 1048576.0).astype(d[k].dtype)
    return d
def setup_inputs_small(rng):
    d = setup_inputs(rng)
    for k in ("x",): d[k] = (d[k].astype(np.float32) * (1 / 1048576.0)).astype(d[k].dtype)
    return d
def setup_inputs_apart(rng):
    d = setup_inputs(rng)
    f = (10.0 ** rng.permutation(np.linspace(-1.5, 1.5, N))).astype(np.float32).reshape(N, 1, 1)
    for k in ("x",): d[k] = (d[k].astype(np.float32) * f).astype(d[k].dtype)
    return d
def reference(x, w):
    X, W = x.astype(np.float64), w.astype(np.float64)
    h = list(X)
    for _ in range(TIMES):
        h = [np.maximum(sum(W[r][:, 128 * i:128 * i + 128].T @ h[j] for i, j in enumerate(MASK[r])), 0.0) for r in range(N)]
    return {"y": np.stack(h).astype(ml_dtypes.bfloat16)}

@@ -1,0 +1,183 @@
+from concourse.bass import DstId, RemoteDMATransfer
+from concourse.mybir import AluOpType
+
+N, TK = 16, 128
+
+SCRATCH = {
+    "W": ("sbuf", [128, N * TK], "bfloat16"),
+    "H1": ("sbuf", [128, N * TK], "bfloat16"),
+    "H2": ("sbuf", [128, N * TK], "bfloat16"),
+    "xd": ("dram", [128, TK], "bfloat16"),
+    "out": ("sbuf", [128, TK], "bfloat16"),
+    "zero": ("sbuf", [128, TK], "float32"),
+    "P1": ("psum", [128, 512], "float32"),
+    "P2": ("psum", [128, 512], "float32"),
+}
+SEMAPHORES = (["xd_in", "x_in", "w_in", "z_in", "mm1", "mm2", "h1", "h2", "y_out", "sent"]
+              + ["a1_%d" % j for j in range(N)] + ["a2_%d" % j for j in range(N)])
+
+SHARE = {
+    1: (0, 1, 0, 0, 3, 2, 1, 0, 0, 2, 0, 3, 0, 1, 2),
+    2: (0, 1, 0, 3, 0, 2, 1, 0, 3, 2, 0, 3, 0, 1, 2),
+}
+LAG = 4
+
+
+def _count(mask):
+    return sum(1 for b in range(mask.bit_length()) if (mask >> b) & 1)
+
+
+def _take(mask, n):
+    got = 0
+    for b in range(mask.bit_length()):
+        if (mask >> b) & 1 and _count(got) < n:
+            got |= 1 << b
+    return got
+
+
+def _pow2(n):
+    p = 1
+    while p * 2 <= n:
+        p *= 2
+    return p
+
+
+def _common(topo, src, dsts):
+    m = topo.mask(src, dsts[0])
+    for d in dsts[1:]:
+        m &= topo.mask(src, d)
+    return m
+
+
+def _team(T, topo, s):
+    me = T.cores[s]
+    world = topo.CORES_PER_HOST * (1 + max(topo.host(c) for c in T.cores))
+    idle = [c for c in range(world)
+            if topo.host(c) == topo.host(me) and topo.chip(c) == topo.chip(me) and T.rank_of(c) is None
+            and all(topo.may_write(c, d) for d in T.cores)]
+    far = [c for c in idle if topo.die(c) != topo.die(me)]
+    near = [c for c in idle if topo.die(c) == topo.die(me)]
+    return [me] + far[:2] + near[:1]
+
+
+def _plan(T, s, rnd):
+    mask = T.tables["MASK"]
+    n = len(T.cores)
+    want = sorted((r for r in range(n) if r != s and s in mask[r]), key=lambda r: (r - s) % n)
+    plan = [[], [], [], []]
+    for k, r in enumerate(want):
+        plan[SHARE[rnd][k % len(SHARE[rnd])]].append(r)
+    return plan
+
+
+def _fan_mask(T, topo, s, rnd):
+    team, plan = _team(T, topo, s), _plan(T, s, rnd)
+    on = _common(topo, team[0], team[1:])
+    if rnd == 1 and plan[0]:
+        rest = on & ~_common(topo, team[0], [T.cores[r] for r in plan[0]])
+        if rest:
+            on = rest
+    return _take(on, _pow2(_count(on)))
+
+
+def rank_program(g, core, T, topo):
+    n = len(T.cores)
+    mask = T.tables["MASK"]
+    sem = T.sem
+    sent = [0]
+
+    def slot(buf, j):
+        return buf[:, j * TK:(j + 1) * TK]
+
+    def send(src, dst, arrive, targets, engines):
+        ids = []
+        for d in targets:
+            rid, pid = topo.addr(d, core)
+            ids.append(DstId(rid=rid, pnc=pid))
+        g.remote_dma_fused([RemoteDMATransfer(dst_ids=ids, dma_engine_mask=engines, remote_sem=arrive, srcs=[src],
+                                              dsts=[dst] * len(ids), alu_op=0)], local_sem=sem.sent)
+        sent[0] += _count(engines)
+
+    def copies(s, k, rnd, src):
+        ranks = _plan(T, s, rnd)[k]
+        if ranks:
+            targets = [T.cores[r] for r in ranks]
+            m = _common(topo, core, targets)
+            send(src, slot(T.H1 if rnd == 1 else T.H2, s), sem["a%d_%d" % (rnd, s)], targets, _take(m, _pow2(_count(m))))
+
+    def hand_over(s, rnd, src, dst):
+        team, plan = _team(T, topo, s), _plan(T, s, rnd)
+        helpers = [team[k] for k in range(1, len(team)) if plan[k]]
+        if helpers:
+            send(src, dst, sem["a%d_%d" % (rnd, s)], helpers, _fan_mask(T, topo, s, rnd))
+
+    rank = T.rank_of(core)
+    if rank is None:
+        for s in range(n):
+            team = _team(T, topo, s)
+            if core in team:
+                k = team.index(core)
+                if _plan(T, s, 1)[k]:
+                    g.wait_ge(sem["a1_%d" % s], _count(_fan_mask(T, topo, s, 1)))
+                    copies(s, k, 1, T.xd[:])
+                if _plan(T, s, 2)[k]:
+                    g.wait_ge(sem["a2_%d" % s], _count(_fan_mask(T, topo, s, 2)))
+                    copies(s, k, 2, slot(T.H2, s))
+                if sent[0]:
+                    g.wait_ge(sem.sent, sent[0])
+        return
+
+    g.sync.dma_start(T.xd[:], T.x[:]).then_inc(sem.xd_in, 16)
+    g.sync.dma_start(slot(T.H1, rank), T.x[:]).then_inc(sem.x_in, 16)
+    g.sync.dma_start(T.W[:], T.w[:]).then_inc(sem.w_in, 16)
+    g.vector.memset(T.zero[:], 0.0).then_inc(sem.z_in, 1)
+
+    g.wait_ge(sem.xd_in, 16)
+    hand_over(rank, 1, T.xd[:], T.xd[:])
+    copies(rank, 0, 1, T.xd[:])
+    g.wait_ge(sem.h1, 1)
+    hand_over(rank, 2, slot(T.H2, rank), slot(T.H2, rank))
+    copies(rank, 0, 2, slot(T.H2, rank))
+
+    def expected(j, rnd):
+        if j == rank:
+            return -1.0
+        plan = _plan(T, j, rnd)
+        for k in range(len(plan)):
+            if rank in plan[k]:
+                return plan[k].index(rank) + (LAG + 0.25 * k if k else 0.0)
+
+    def arrival(j, rnd):
+        team, plan = _team(T, topo, j), _plan(T, j, rnd)
+        for k in range(len(plan)):
+            if rank in plan[k]:
+                m = _common(topo, team[k], [T.cores[r] for r in plan[k]])
+                return _pow2(_count(m))
+
+    g.tensor.wait_ge(sem.w_in, 16)
+    for rnd, H, P, done in ((1, T.H1, T.P1, sem.mm1), (2, T.H2, T.P2, sem.mm2)):
+        tiles = sorted(range(len(mask[rank])), key=lambda i: (expected(mask[rank][i], rnd), i))
+        seen = []
+        for pos, i in enumerate(tiles):
+            j = mask[rank][i]
+            if j not in seen:
+                seen.append(j)
+                if j != rank:
+                    g.tensor.wait_ge(sem["a%d_%d" % (rnd, j)], arrival(j, rnd))
+                elif rnd == 1:
+                    g.tensor.wait_ge(sem.x_in, 16)
+                else:
+                    g.tensor.wait_ge(sem.h1, 1)
+            mm = g.tensor.matmul(P[:, 0:TK], slot(T.W, i), slot(H, j), pos == 0, pos == len(tiles) - 1)
+        mm.then_inc(done, 1)
+
+    g.vector.wait_ge(sem.z_in, 1)
+    g.vector.wait_ge(sem.mm1, 1)
+    g.vector.tensor_tensor(slot(T.H2, rank), T.P1[:, 0:TK], T.zero[:], AluOpType.max).then_inc(sem.h1, 1)
+    g.vector.wait_ge(sem.mm2, 1)
+    g.vector.tensor_tensor(T.out[:], T.P2[:, 0:TK], T.zero[:], AluOpType.max).then_inc(sem.h2, 1)
+
+    g.sync.wait_ge(sem.h2, 1)
+    g.sync.dma_start(T.y[:], T.out[:]).then_inc(sem.y_out, 16)
+    g.sync.wait_ge(sem.y_out, 16)
+    g.wait_ge(sem.sent, sent[0])

@@ -2,19 +2,24 @@ from concourse.bass import DstId, RemoteDMATransfer
 from concourse.mybir import AluOpType
 
 N, TK = 16, 128
+NH = 2
+HW = TK // NH
 
 SCRATCH = {
     "W": ("sbuf", [128, N * TK], "bfloat16"),
     "H1": ("sbuf", [128, N * TK], "bfloat16"),
     "H2": ("sbuf", [128, N * TK], "bfloat16"),
-    "xd": ("dram", [128, TK], "bfloat16"),
+    "xd": ("dram", [NH, 128, HW], "bfloat16"),
     "out": ("sbuf", [128, TK], "bfloat16"),
-    "zero": ("sbuf", [128, TK], "float32"),
-    "P1": ("psum", [128, 512], "float32"),
-    "P2": ("psum", [128, 512], "float32"),
+    "zero": ("sbuf", [128, HW], "float32"),
+    "P1_0": ("psum", [128, 512], "float32"),
+    "P1_1": ("psum", [128, 512], "float32"),
+    "P2_0": ("psum", [128, 512], "float32"),
+    "P2_1": ("psum", [128, 512], "float32"),
 }
-SEMAPHORES = (["xd_in", "x_in", "w_in", "z_in", "mm1", "mm2", "h1", "h2", "y_out", "sent"]
-              + ["a1_%d" % j for j in range(N)] + ["a2_%d" % j for j in range(N)])
+SEMAPHORES = (["x_in", "w_in", "z_in", "sent"]
+              + ["%s_%d" % (nm, q) for nm in ("xd_in", "mm1", "mm2", "h1", "h2", "y_out") for q in range(NH)]
+              + ["a%d_%d_%d" % (rnd, q, j) for rnd in (1, 2) for q in range(NH) for j in range(N)])
 
 SHARE = {
     1: (0, 1, 0, 0, 3, 2, 1, 0, 0, 2, 0, 3, 0, 1, 2),
@@ -73,7 +78,7 @@ def _plan(T, s, rnd):
 def _fan_mask(T, topo, s, rnd):
     team, plan = _team(T, topo, s), _plan(T, s, rnd)
     on = _common(topo, team[0], team[1:])
-    if rnd == 1 and plan[0]:
+    if plan[0]:
         rest = on & ~_common(topo, team[0], [T.cores[r] for r in plan[0]])
         if rest:
             on = rest
@@ -89,6 +94,12 @@ def rank_program(g, core, T, topo):
     def slot(buf, j):
         return buf[:, j * TK:(j + 1) * TK]
 
+    def half(buf, j, q):
+        return buf[:, j * TK + q * HW:j * TK + (q + 1) * HW]
+
+    def arr(rnd, q, j):
+        return sem["a%d_%d_%d" % (rnd, q, j)]
+
     def send(src, dst, arrive, targets, engines):
         ids = []
         for d in targets:
@@ -98,18 +109,22 @@ def rank_program(g, core, T, topo):
                                               dsts=[dst] * len(ids), alu_op=0)], local_sem=sem.sent)
         sent[0] += _count(engines)
 
-    def copies(s, k, rnd, src):
+    def source(s, rnd, q):
+        return T.xd[q] if rnd == 1 else half(T.H2, s, q)
+
+    def copies(s, k, rnd, q):
         ranks = _plan(T, s, rnd)[k]
         if ranks:
             targets = [T.cores[r] for r in ranks]
             m = _common(topo, core, targets)
-            send(src, slot(T.H1 if rnd == 1 else T.H2, s), sem["a%d_%d" % (rnd, s)], targets, _take(m, _pow2(_count(m))))
+            send(source(s, rnd, q), half(T.H1 if rnd == 1 else T.H2, s, q), arr(rnd, q, s), targets,
+                 _take(m, _pow2(_count(m))))
 
-    def hand_over(s, rnd, src, dst):
+    def hand_over(s, rnd, q):
         team, plan = _team(T, topo, s), _plan(T, s, rnd)
         helpers = [team[k] for k in range(1, len(team)) if plan[k]]
         if helpers:
-            send(src, dst, sem["a%d_%d" % (rnd, s)], helpers, _fan_mask(T, topo, s, rnd))
+            send(source(s, rnd, q), source(s, rnd, q), arr(rnd, q, s), helpers, _fan_mask(T, topo, s, rnd))
 
     rank = T.rank_of(core)
     if rank is None:
@@ -117,27 +132,29 @@ def rank_program(g, core, T, topo):
             team = _team(T, topo, s)
             if core in team:
                 k = team.index(core)
-                if _plan(T, s, 1)[k]:
-                    g.wait_ge(sem["a1_%d" % s], _count(_fan_mask(T, topo, s, 1)))
-                    copies(s, k, 1, T.xd[:])
-                if _plan(T, s, 2)[k]:
-                    g.wait_ge(sem["a2_%d" % s], _count(_fan_mask(T, topo, s, 2)))
-                    copies(s, k, 2, slot(T.H2, s))
+                for rnd in (1, 2):
+                    if _plan(T, s, rnd)[k]:
+                        for q in range(NH):
+                            g.wait_ge(arr(rnd, q, s), _count(_fan_mask(T, topo, s, rnd)))
+                            copies(s, k, rnd, q)
                 if sent[0]:
                     g.wait_ge(sem.sent, sent[0])
         return
 
-    g.sync.dma_start(T.xd[:], T.x[:]).then_inc(sem.xd_in, 16)
+    for q in range(NH):
+        g.sync.dma_start(T.xd[q], T.x[:, q * HW:(q + 1) * HW]).then_inc(sem["xd_in_%d" % q], 16)
     g.sync.dma_start(slot(T.H1, rank), T.x[:]).then_inc(sem.x_in, 16)
     g.sync.dma_start(T.W[:], T.w[:]).then_inc(sem.w_in, 16)
     g.vector.memset(T.zero[:], 0.0).then_inc(sem.z_in, 1)
 
-    g.wait_ge(sem.xd_in, 16)
-    hand_over(rank, 1, T.xd[:], T.xd[:])
-    copies(rank, 0, 1, T.xd[:])
-    g.wait_ge(sem.h1, 1)
-    hand_over(rank, 2, slot(T.H2, rank), slot(T.H2, rank))
-    copies(rank, 0, 2, slot(T.H2, rank))
+    for rnd in (1, 2):
+        for q in range(NH):
+            if rnd == 1:
+                g.wait_ge(sem["xd_in_%d" % q], 16)
+            else:
+                g.wait_ge(sem["h1_%d" % q], 1)
+            hand_over(rank, rnd, q)
+            copies(rank, 0, rnd, q)
 
     def expected(j, rnd):
         if j == rank:
@@ -155,29 +172,35 @@ def rank_program(g, core, T, topo):
                 return _pow2(_count(m))
 
     g.tensor.wait_ge(sem.w_in, 16)
-    for rnd, H, P, done in ((1, T.H1, T.P1, sem.mm1), (2, T.H2, T.P2, sem.mm2)):
+    for rnd, H in ((1, T.H1), (2, T.H2)):
         tiles = sorted(range(len(mask[rank])), key=lambda i: (expected(mask[rank][i], rnd), i))
-        seen = []
-        for pos, i in enumerate(tiles):
-            j = mask[rank][i]
-            if j not in seen:
-                seen.append(j)
-                if j != rank:
-                    g.tensor.wait_ge(sem["a%d_%d" % (rnd, j)], arrival(j, rnd))
-                elif rnd == 1:
-                    g.tensor.wait_ge(sem.x_in, 16)
-                else:
-                    g.tensor.wait_ge(sem.h1, 1)
-            mm = g.tensor.matmul(P[:, 0:TK], slot(T.W, i), slot(H, j), pos == 0, pos == len(tiles) - 1)
-        mm.then_inc(done, 1)
+        for q in range(NH):
+            P = T["P%d_%d" % (rnd, q)]
+            seen = []
+            for pos, i in enumerate(tiles):
+                j = mask[rank][i]
+                if j not in seen:
+                    seen.append(j)
+                    if j != rank:
+                        g.tensor.wait_ge(arr(rnd, q, j), arrival(j, rnd))
+                    elif rnd == 1:
+                        g.tensor.wait_ge(sem.x_in, 16)
+                    else:
+                        g.tensor.wait_ge(sem["h1_%d" % q], 1)
+                mm = g.tensor.matmul(P[:, 0:HW], slot(T.W, i), half(H, j, q), pos == 0, pos == len(tiles) - 1)
+            mm.then_inc(sem["mm%d_%d" % (rnd, q)], 1)
 
     g.vector.wait_ge(sem.z_in, 1)
-    g.vector.wait_ge(sem.mm1, 1)
-    g.vector.tensor_tensor(slot(T.H2, rank), T.P1[:, 0:TK], T.zero[:], AluOpType.max).then_inc(sem.h1, 1)
-    g.vector.wait_ge(sem.mm2, 1)
-    g.vector.tensor_tensor(T.out[:], T.P2[:, 0:TK], T.zero[:], AluOpType.max).then_inc(sem.h2, 1)
+    for rnd in (1, 2):
+        for q in range(NH):
+            g.vector.wait_ge(sem["mm%d_%d" % (rnd, q)], 1)
+            res = half(T.H2, rank, q) if rnd == 1 else T.out[:, q * HW:(q + 1) * HW]
+            g.vector.tensor_tensor(res, T["P%d_%d" % (rnd, q)][:, 0:HW], T.zero[:],
+                                   AluOpType.max).then_inc(sem["h%d_%d" % (rnd, q)], 1)
 
-    g.sync.wait_ge(sem.h2, 1)
-    g.sync.dma_start(T.y[:], T.out[:]).then_inc(sem.y_out, 16)
-    g.sync.wait_ge(sem.y_out, 16)
+    for q in range(NH):
+        g.sync.wait_ge(sem["h2_%d" % q], 1)
+        g.sync.dma_start(T.y[:, q * HW:(q + 1) * HW], T.out[:, q * HW:(q + 1) * HW]).then_inc(sem["y_out_%d" % q], 16)
+    for q in range(NH):
+        g.sync.wait_ge(sem["y_out_%d" % q], 16)
     g.wait_ge(sem.sent, sent[0])

from concourse.bass import DstId, RemoteDMATransfer
from concourse.mybir import AluOpType

N, TK = 16, 128
NH = 2
HW = TK // NH

SCRATCH = {
    "W": ("sbuf", [128, N * TK], "bfloat16"),
    "H1": ("sbuf", [128, N * TK], "bfloat16"),
    "H2": ("sbuf", [128, N * TK], "bfloat16"),
    "xd": ("dram", [NH, 128, HW], "bfloat16"),
    "out": ("sbuf", [128, TK], "bfloat16"),
    "zero": ("sbuf", [128, HW], "float32"),
    "P1_0": ("psum", [128, 512], "float32"),
    "P1_1": ("psum", [128, 512], "float32"),
    "P2_0": ("psum", [128, 512], "float32"),
    "P2_1": ("psum", [128, 512], "float32"),
}
SEMAPHORES = (["x_in", "w_in", "z_in", "sent"]
              + ["%s_%d" % (nm, q) for nm in ("xd_in", "mm1", "mm2", "h1", "h2", "y_out") for q in range(NH)]
              + ["a%d_%d_%d" % (rnd, q, j) for rnd in (1, 2) for q in range(NH) for j in range(N)])

SHARE = {
    1: (0, 1, 0, 0, 3, 2, 1, 0, 0, 2, 0, 3, 0, 1, 2),
    2: (0, 1, 0, 3, 0, 2, 1, 0, 3, 2, 0, 3, 0, 1, 2),
}
LAG = 4


def _count(mask):
    return sum(1 for b in range(mask.bit_length()) if (mask >> b) & 1)


def _take(mask, n):
    got = 0
    for b in range(mask.bit_length()):
        if (mask >> b) & 1 and _count(got) < n:
            got |= 1 << b
    return got


def _pow2(n):
    p = 1
    while p * 2 <= n:
        p *= 2
    return p


def _common(topo, src, dsts):
    m = topo.mask(src, dsts[0])
    for d in dsts[1:]:
        m &= topo.mask(src, d)
    return m


def _team(T, topo, s):
    me = T.cores[s]
    world = topo.CORES_PER_HOST * (1 + max(topo.host(c) for c in T.cores))
    idle = [c for c in range(world)
            if topo.host(c) == topo.host(me) and topo.chip(c) == topo.chip(me) and T.rank_of(c) is None
            and all(topo.may_write(c, d) for d in T.cores)]
    far = [c for c in idle if topo.die(c) != topo.die(me)]
    near = [c for c in idle if topo.die(c) == topo.die(me)]
    return [me] + far[:2] + near[:1]


def _plan(T, s, rnd):
    mask = T.tables["MASK"]
    n = len(T.cores)
    want = sorted((r for r in range(n) if r != s and s in mask[r]), key=lambda r: (r - s) % n)
    plan = [[], [], [], []]
    for k, r in enumerate(want):
        plan[SHARE[rnd][k % len(SHARE[rnd])]].append(r)
    return plan


def _fan_mask(T, topo, s, rnd):
    team, plan = _team(T, topo, s), _plan(T, s, rnd)
    on = _common(topo, team[0], team[1:])
    if plan[0]:
        rest = on & ~_common(topo, team[0], [T.cores[r] for r in plan[0]])
        if rest:
            on = rest
    return _take(on, _pow2(_count(on)))


def rank_program(g, core, T, topo):
    n = len(T.cores)
    mask = T.tables["MASK"]
    sem = T.sem
    sent = [0]

    def slot(buf, j):
        return buf[:, j * TK:(j + 1) * TK]

    def half(buf, j, q):
        return buf[:, j * TK + q * HW:j * TK + (q + 1) * HW]

    def arr(rnd, q, j):
        return sem["a%d_%d_%d" % (rnd, q, j)]

    def send(src, dst, arrive, targets, engines):
        ids = []
        for d in targets:
            rid, pid = topo.addr(d, core)
            ids.append(DstId(rid=rid, pnc=pid))
        g.remote_dma_fused([RemoteDMATransfer(dst_ids=ids, dma_engine_mask=engines, remote_sem=arrive, srcs=[src],
                                              dsts=[dst] * len(ids), alu_op=0)], local_sem=sem.sent)
        sent[0] += _count(engines)

    def source(s, rnd, q):
        return T.xd[q] if rnd == 1 else half(T.H2, s, q)

    def copies(s, k, rnd, q):
        ranks = _plan(T, s, rnd)[k]
        if ranks:
            targets = [T.cores[r] for r in ranks]
            m = _common(topo, core, targets)
            send(source(s, rnd, q), half(T.H1 if rnd == 1 else T.H2, s, q), arr(rnd, q, s), targets,
                 _take(m, _pow2(_count(m))))

    def hand_over(s, rnd, q):
        team, plan = _team(T, topo, s), _plan(T, s, rnd)
        helpers = [team[k] for k in range(1, len(team)) if plan[k]]
        if helpers:
            send(source(s, rnd, q), source(s, rnd, q), arr(rnd, q, s), helpers, _fan_mask(T, topo, s, rnd))

    rank = T.rank_of(core)
    if rank is None:
        for s in range(n):
            team = _team(T, topo, s)
            if core in team:
                k = team.index(core)
                for rnd in (1, 2):
                    if _plan(T, s, rnd)[k]:
                        for q in range(NH):
                            g.wait_ge(arr(rnd, q, s), _count(_fan_mask(T, topo, s, rnd)))
                            copies(s, k, rnd, q)
                if sent[0]:
                    g.wait_ge(sem.sent, sent[0])
        return

    for q in range(NH):
        g.sync.dma_start(T.xd[q], T.x[:, q * HW:(q + 1) * HW]).then_inc(sem["xd_in_%d" % q], 16)
    g.sync.dma_start(slot(T.H1, rank), T.x[:]).then_inc(sem.x_in, 16)
    g.sync.dma_start(T.W[:], T.w[:]).then_inc(sem.w_in, 16)
    g.vector.memset(T.zero[:], 0.0).then_inc(sem.z_in, 1)

    for rnd in (1, 2):
        for q in range(NH):
            if rnd == 1:
                g.wait_ge(sem["xd_in_%d" % q], 16)
            else:
                g.wait_ge(sem["h1_%d" % q], 1)
            hand_over(rank, rnd, q)
            copies(rank, 0, rnd, q)

    def expected(j, rnd):
        if j == rank:
            return -1.0
        plan = _plan(T, j, rnd)
        for k in range(len(plan)):
            if rank in plan[k]:
                return plan[k].index(rank) + (LAG + 0.25 * k if k else 0.0)

    def arrival(j, rnd):
        team, plan = _team(T, topo, j), _plan(T, j, rnd)
        for k in range(len(plan)):
            if rank in plan[k]:
                m = _common(topo, team[k], [T.cores[r] for r in plan[k]])
                return _pow2(_count(m))

    g.tensor.wait_ge(sem.w_in, 16)
    for rnd, H in ((1, T.H1), (2, T.H2)):
        tiles = sorted(range(len(mask[rank])), key=lambda i: (expected(mask[rank][i], rnd), i))
        for q in range(NH):
            P = T["P%d_%d" % (rnd, q)]
            seen = []
            for pos, i in enumerate(tiles):
                j = mask[rank][i]
                if j not in seen:
                    seen.append(j)
                    if j != rank:
                        g.tensor.wait_ge(arr(rnd, q, j), arrival(j, rnd))
                    elif rnd == 1:
                        g.tensor.wait_ge(sem.x_in, 16)
                    else:
                        g.tensor.wait_ge(sem["h1_%d" % q], 1)
                mm = g.tensor.matmul(P[:, 0:HW], slot(T.W, i), half(H, j, q), pos == 0, pos == len(tiles) - 1)
            mm.then_inc(sem["mm%d_%d" % (rnd, q)], 1)

    g.vector.wait_ge(sem.z_in, 1)
    for rnd in (1, 2):
        for q in range(NH):
            g.vector.wait_ge(sem["mm%d_%d" % (rnd, q)], 1)
            res = half(T.H2, rank, q) if rnd == 1 else T.out[:, q * HW:(q + 1) * HW]
            g.vector.tensor_tensor(res, T["P%d_%d" % (rnd, q)][:, 0:HW], T.zero[:],
                                   AluOpType.max).then_inc(sem["h%d_%d" % (rnd, q)], 1)

    for q in range(NH):
        g.sync.wait_ge(sem["h2_%d" % q], 1)
        g.sync.dma_start(T.y[:, q * HW:(q + 1) * HW], T.out[:, q * HW:(q + 1) * HW]).then_inc(sem["y_out_%d" % q], 16)
    for q in range(NH):
        g.sync.wait_ge(sem["y_out_%d" % q], 16)
    g.wait_ge(sem.sent, sent[0])
